import numpy as np
import ml_dtypes


def mxq(x, axis, fmt="e4m3"):
    dtype, down = {"e4m3": (ml_dtypes.float8_e4m3fn, 7), "e5m2": (ml_dtypes.float8_e5m2, 14)}[fmt]
    v = np.moveaxis(np.asarray(x, np.float32).astype(ml_dtypes.bfloat16).astype(np.float64), axis, -1)
    blocks = v.reshape(v.shape[:-1] + (-1, 32))
    amax = np.abs(blocks).max(-1, keepdims=True)
    byte = np.maximum(np.where(amax > 0, np.frexp(amax)[1] - 1 + 127, 0) - down, 1)
    scale = np.exp2(byte - 127.0)
    codes = (blocks / scale).astype(np.float32).astype(dtype).astype(np.float64)
    return np.moveaxis((codes * scale).reshape(v.shape), -1, axis)


WIDE = False


def mx_kscale(k):
    if not WIDE:
        return np.ones(k)
    levels = np.array([10, -10, 5, -5, 0])
    if k % 512:
        return np.exp2(np.random.permutation(np.resize(levels, k // 32))).repeat(32)
    a = np.empty((k // 512, 16))
    for p in range(k // 512):
        a[p, :8] = np.random.permutation(np.resize(levels, 8))
        for g in range(8):
            far = levels[np.abs(levels - a[p, g]) >= 10]
            a[p, g + 8] = far[np.random.randint(len(far))]
    return np.exp2(a.ravel()).repeat(32)


def f64(x):
    return np.asarray(x).astype(np.float64)


def striped(idx):
    return np.tile(idx.reshape(-1, 16).T, (8, 1)).astype(np.uint16)


def unstriped(offs):
    return offs[:16].T.reshape(-1).astype(np.int64)


E2M1 = np.array([0.0, 0.5, 1.0, 1.5, 2.0, 3.0, 4.0, 6.0, -0.0, -0.5, -1.0, -1.5, -2.0, -3.0, -4.0, -6.0])


def pack_weight(w, fmt):
    k, n = w.shape
    w = f64(np.asarray(w, np.float32).astype(ml_dtypes.bfloat16)).reshape(k // 32, 32, n)
    amax = np.abs(w).max(1)
    if fmt == "e4m3":
        byte = np.frexp(amax)[1] - 1 + 127 - 7
    else:
        mant, ex = np.frexp(amax / 6.0)
        byte = np.where(mant > 0.5, ex, ex - 1) + 127
    byte = np.clip(np.where(amax > 0, byte, 1), 1, 254)
    scaled = (w * np.exp2(127.0 - byte)[:, None, :]).reshape(k, n).astype(np.float32)
    by_word = np.ascontiguousarray(scaled.reshape(k // 512, 128, 4, n).transpose(0, 1, 3, 2))
    if fmt == "e4m3":
        words = by_word.astype(ml_dtypes.float8_e4m3fn).view(np.uint8)
    else:
        c = by_word.astype(ml_dtypes.float4_e2m1fn).view(np.uint8) & 0xF
        words = (c[..., 0::2] | (c[..., 1::2] << 4)).reshape(k // 512, 128, 2 * n)
    return np.ascontiguousarray(words), np.ascontiguousarray(byte.astype(np.uint8).reshape(k // 512, 16, n))


def unpack_weight(words, scales, fmt):
    g, _, n = scales.shape
    words = np.ascontiguousarray(words).reshape(g, 128, n, -1)
    if fmt == "e4m3":
        vals = words.view(ml_dtypes.float8_e4m3fn).astype(np.float64)
    else:
        nib = np.empty((g, 128, n, 4), np.uint8)
        nib[..., 0::2] = words & 0xF
        nib[..., 1::2] = words >> 4
        vals = E2M1[nib]
    vals = vals * np.repeat(np.exp2(scales.astype(np.float64) - 127.0), 8, axis=1)[..., None]
    return vals.transpose(0, 1, 3, 2).reshape(g * 512, n)


def silu(v):
    return v / (1.0 + np.exp(-np.maximum(v, -700.0)))


K, T, E, C, H, N = 1536, 1024, 4, 128, 512, 128


def by_expert(wq, xq):
    return np.concatenate([wq[e].T @ xq[:, e * C:(e + 1) * C] for e in range(E)], axis=1)


def setup_inputs():
    n = np.random.standard_normal
    s = mx_kscale(K)[:, None]
    u = mx_kscale(H)
    x = pack_weight(n((K, T)) * s, "e4m3")
    return {
        "x_words": x[0],
        "x_scales": x[1],
        "w1": (n((E, K, H)) / np.sqrt(K) / s[None] * u[None, None, :]).astype(np.float32),
        "w2": (n((E, H, N)) / np.sqrt(H) / u[None, :, None]).astype(np.float32),
        "gate": np.tile(np.random.uniform(0.2, 1.0, E * C), (N, 1)).astype(np.float32),
        "offs": striped(np.random.permutation(T)[:E * C]),
    }


def reference(x_words, x_scales, w1, w2, gate, offs):
    idx = unstriped(offs)
    xq = unpack_weight(x_words, x_scales, "e4m3")[:, idx]
    h = silu(by_expert(mxq(f64(w1), 1, "e4m3"), xq))
    y = by_expert(mxq(f64(w2), 1, "e4m3"), mxq(h, 0, "e4m3"))
    out = np.zeros((N, T))
    out[:, idx] = f64(gate) * y
    return out

@@ -1,0 +1,133 @@
+from contextlib import ExitStack
+
+import concourse.mybir as mybir
+from concourse.masks import make_identity
+
+K, T, E, C, H, N = 1536, 1024, 4, 128, 512, 128
+FLOPS = 2 * E * C * (K * H + H * N)
+
+F32 = mybir.dt.float32
+BF16 = mybir.dt.bfloat16
+I32 = mybir.dt.int32
+U32 = mybir.dt.uint32
+U16 = mybir.dt.uint16
+U8 = mybir.dt.uint8
+FP8X4 = mybir.dt.float8_e4m3fn_x4
+
+P = 128
+PACK = 4
+K_PASS = P * PACK
+PASSES = K // K_PASS
+SLOTS = E * C
+LIST_COLS = C // 16
+
+
+def tile_moe_pkd_mlp_silu_kernel(tc, x_words, x_scales, w1, w2, gate, offs, out):
+    nc = tc.nc
+    with ExitStack() as ctx:
+        keep = ctx.enter_context(tc.tile_pool(name="keep", bufs=1))
+        ring = ctx.enter_context(tc.tile_pool(name="ring", bufs=4))
+        psum = ctx.enter_context(tc.psum_pool(name="psum", bufs=1))
+
+        offsets = keep.tile([P, SLOTS // 16], U16, name="offsets")
+        planes = keep.tile([P, T], U8, name="planes", align_bytes=64)
+        window = keep.tile([P, T], F32, name="window")
+        ident = keep.tile([P, P], F32, name="ident")
+        gate_col = keep.tile([P, PACK], F32, name="gate_col")
+        gate_rows = keep.tile([P, SLOTS], F32, name="gate_rows")
+        words = [keep.tile([P, T], U32, name="words%d" % o, align_bytes=64) for o in range(PASSES)]
+        slot_words = [keep.tile([P, SLOTS], U32, name="slot_words%d" % o, align_bytes=64) for o in range(PASSES)]
+        slot_planes = keep.tile([P, SLOTS], U8, name="slot_planes", align_bytes=64)
+        w1_raw = {}
+        w2_raw = {}
+
+        def load_words(o):
+            nc.sync.dma_start(out=words[o][:].bitcast(I32), in_=x_words[o].rearrange("p t r -> p (t r)").bitcast(I32))
+
+        def load_w1(e, o):
+            w1_raw[e, o] = keep.tile([P, PACK, H], F32, name="w1_raw%d_%d" % (e, o))
+            nc.sync.dma_start(out=w1_raw[e, o][:], in_=w1[e, o * K_PASS:(o + 1) * K_PASS, :].rearrange("(p j) c -> p j c", j=PACK))
+
+        def load_w2(e):
+            w2_raw[e] = keep.tile([P, PACK, N], F32, name="w2_raw%d" % e)
+            nc.sync.dma_start(out=w2_raw[e][:], in_=w2[e].rearrange("(p j) n -> p j n", j=PACK))
+
+        nc.gpsimd.memset(planes[:].bitcast(I32), 0)
+        nc.scalar.dma_start(out=gate_col[:], in_=gate[0:1, :].rearrange("o (p j) -> (o p) j", j=PACK))
+        load_words(0)
+        nc.sync.dma_start(offsets[:], offs)
+        for e in range(E):
+            for o in range(PASSES):
+                load_w1(e, o)
+                if e == 0 and o == 0:
+                    for q in range(4):
+                        nc.sync.dma_start(out=planes[32 * q:32 * q + 4 * PASSES, :].bitcast(I32), in_=x_scales[:, 4 * q:4 * q + 4, :].bitcast(I32))
+                if e == 0 and o + 1 < PASSES:
+                    load_words(o + 1)
+            load_w2(e)
+
+        nc.vector.memset(window[:], 0.0)
+        make_identity(nc, ident[:])
+        gate_ps = psum.tile([P, PACK, P], F32, name="gate_ps")
+        for j in range(PACK):
+            nc.tensor.transpose(gate_ps[:, j, :], gate_col[:, j:j + 1].to_broadcast([P, P]), ident[:])
+        nc.scalar.copy(out=gate_rows[:].rearrange("p (s j) -> p s j", j=PACK), in_=gate_ps[:].rearrange("p j s -> p s j"))
+
+        def gather_words(o):
+            nc.vector.tensor_copy(slot_words[o][:], words[o][:].indirect(offsets[:]))
+
+        def first_layer_pass(e, o, acc):
+            src = w1_raw[e, o][:].rearrange("p j (m t) -> p m j t", t=PACK)
+            grouped = []
+            for half in range(2):
+                g = ring.tile([P, 2, P, PACK], BF16, name="w1_grouped%d" % half, align_bytes=64)
+                dst = g[:].rearrange("p t m j -> p m j t")
+                if half == 0:
+                    nc.vector.tensor_copy(out=dst, in_=src[:, :, :, 0:2])
+                else:
+                    nc.scalar.copy(out=dst, in_=src[:, :, :, 2:4])
+                grouped.append(g)
+            for half in range(2):
+                codes = ring.tile([P, 2 * P], U32, name="w1_codes%d" % half, align_bytes=64)
+                scales = ring.tile([P, 2 * P], U8, name="w1_scales%d" % half, align_bytes=64)
+                nc.vector.quantize_mx(out=codes[:].bitcast(FP8X4), scales=scales[:], in_=grouped[half][:].rearrange("p t m j -> p (t m j)"))
+                for tt in range(2):
+                    cols = slice(tt * P, (tt + 1) * P)
+                    slots = slice(e * C, (e + 1) * C)
+                    nc.tensor.matmul_mx(
+                        out=acc[2 * half + tt][:],
+                        lhsT=codes[:, cols].bitcast(FP8X4), lhsT_scale=scales[:, cols],
+                        rhs=slot_words[o][:, slots].bitcast(FP8X4), rhs_scale=slot_planes[4 * o:P, slots],
+                        start=(o == 0), stop=(o == PASSES - 1))
+
+        def second_layer(e, acc):
+            w2_grouped = ring.tile([P, N, PACK], BF16, name="w2_grouped", align_bytes=64)
+            nc.scalar.copy(out=w2_grouped[:].rearrange("p (c i) j -> p c j i", i=4), in_=w2_raw[e][:].rearrange("p j (c i) -> p c j i", i=4))
+            w2_codes = ring.tile([P, N], U32, name="w2_codes", align_bytes=64)
+            w2_scales = ring.tile([P, N], U8, name="w2_scales", align_bytes=64)
+            nc.vector.quantize_mx(out=w2_codes[:].bitcast(FP8X4), scales=w2_scales[:], in_=w2_grouped[:].rearrange("p n j -> p (n j)"))
+            h = ring.tile([P, PACK, C], BF16, name="h", align_bytes=64)
+            for t in range(PACK):
+                nc.scalar.activation(out=h[:, t, :], in_=acc[t][:], func=mybir.ActivationFunctionType.Silu)
+            h_grouped = ring.tile([P, C, PACK], BF16, name="h_grouped", align_bytes=64)
+            nc.vector.tensor_copy(out=h_grouped[:].rearrange("p (c i) t -> p c t i", i=4), in_=h[:].rearrange("p t (c i) -> p c t i", i=4))
+            h_codes = ring.tile([P, C], U32, name="h_codes", align_bytes=64)
+            h_scales = ring.tile([P, C], U8, name="h_scales", align_bytes=64)
+            nc.vector.quantize_mx(out=h_codes[:].bitcast(FP8X4), scales=h_scales[:], in_=h_grouped[:].rearrange("p c t -> p (c t)"))
+            y_ps = psum.tile([P, C], F32, name="y_ps", bufs=2)
+            nc.tensor.matmul_mx(out=y_ps[:], lhsT=w2_codes[:].bitcast(FP8X4), lhsT_scale=w2_scales[:],
+                                rhs=h_codes[:].bitcast(FP8X4), rhs_scale=h_scales[:], start=True, stop=True)
+            y = ring.tile([P, C], F32, name="y")
+            nc.scalar.copy(out=y[:], in_=y_ps[:])
+            nc.vector.tensor_tensor(window[:].indirect(offsets[:, e * LIST_COLS:(e + 1) * LIST_COLS]), y[:], gate_rows[:, e * C:(e + 1) * C], mybir.AluOpType.mult)
+
+        for e in range(E):
+            acc = [psum.tile([P, C], F32, name="acc%d" % t) for t in range(PACK)]
+            for o in range(PASSES):
+                if e == 0:
+                    gather_words(o)
+                    if o == 0:
+                        nc.vector.tensor_copy(slot_planes[:], planes[:].indirect(offsets[:]))
+                first_layer_pass(e, o, acc)
+            second_layer(e, acc)
+        nc.sync.dma_start(out=out, in_=window[:])

@@ -45,8 +45,14 @@ def tile_moe_pkd_mlp_silu_kernel(tc, x_words, x_scales, w1, w2, gate, offs, out)
             nc.sync.dma_start(out=words[o][:].bitcast(I32), in_=x_words[o].rearrange("p t r -> p (t r)").bitcast(I32))
 
         def load_w1(e, o):
-            w1_raw[e, o] = keep.tile([P, PACK, H], F32, name="w1_raw%d_%d" % (e, o))
-            nc.sync.dma_start(out=w1_raw[e, o][:], in_=w1[e, o * K_PASS:(o + 1) * K_PASS, :].rearrange("(p j) c -> p j c", j=PACK))
+            pieces = 2 if (e, o) == (E - 1, PASSES - 1) else 1
+            width = H // pieces
+            rows = w1[e, o * K_PASS:(o + 1) * K_PASS, :].rearrange("(p j) c -> p j c", j=PACK)
+            w1_raw[e, o] = []
+            for u in range(pieces):
+                raw = keep.tile([P, PACK, width], F32, name="w1_raw%d_%d_%d" % (e, o, u), tag="raw%d_%d_%d" % (e, o, u), align_bytes=64)
+                nc.sync.dma_start(out=raw[:], in_=rows[:, :, u * width:(u + 1) * width])
+                w1_raw[e, o].append(raw)
 
         def load_w2(e):
             w2_raw[e] = keep.tile([P, PACK, N], F32, name="w2_raw%d" % e)
@@ -77,57 +83,90 @@ def tile_moe_pkd_mlp_silu_kernel(tc, x_words, x_scales, w1, w2, gate, offs, out)
             nc.vector.tensor_copy(slot_words[o][:], words[o][:].indirect(offsets[:]))
 
         def first_layer_pass(e, o, acc):
-            src = w1_raw[e, o][:].rearrange("p j (m t) -> p m j t", t=PACK)
-            grouped = []
-            for half in range(2):
-                g = ring.tile([P, 2, P, PACK], BF16, name="w1_grouped%d" % half, align_bytes=64)
-                dst = g[:].rearrange("p t m j -> p m j t")
-                if half == 0:
-                    nc.vector.tensor_copy(out=dst, in_=src[:, :, :, 0:2])
-                else:
-                    nc.scalar.copy(out=dst, in_=src[:, :, :, 2:4])
-                grouped.append(g)
-            for half in range(2):
-                codes = ring.tile([P, 2 * P], U32, name="w1_codes%d" % half, align_bytes=64)
-                scales = ring.tile([P, 2 * P], U8, name="w1_scales%d" % half, align_bytes=64)
-                nc.vector.quantize_mx(out=codes[:].bitcast(FP8X4), scales=scales[:], in_=grouped[half][:].rearrange("p t m j -> p (t m j)"))
-                for tt in range(2):
-                    cols = slice(tt * P, (tt + 1) * P)
-                    slots = slice(e * C, (e + 1) * C)
-                    nc.tensor.matmul_mx(
-                        out=acc[2 * half + tt][:],
-                        lhsT=codes[:, cols].bitcast(FP8X4), lhsT_scale=scales[:, cols],
-                        rhs=slot_words[o][:, slots].bitcast(FP8X4), rhs_scale=slot_planes[4 * o:P, slots],
-                        start=(o == 0), stop=(o == PASSES - 1))
+            grouped = ring.tile([P, PACK, P, PACK], BF16, name="w1_grouped", align_bytes=64)
+            pieces = len(w1_raw[e, o])
+            for u, raw in enumerate(w1_raw[e, o]):
+                src = raw[:].rearrange("p j (m t) -> p m j t", t=PACK)
+                dst = grouped[:, :, u * P // pieces:(u + 1) * P // pieces, :].rearrange("p t m j -> p m j t")
+                nc.vector.tensor_copy(out=dst[:, :, :, 0:2], in_=src[:, :, :, 0:2])
+                nc.scalar.copy(out=dst[:, :, :, 2:4], in_=src[:, :, :, 2:4])
+            codes = ring.tile([P, H], U32, name="w1_codes", align_bytes=64, bufs=6)
+            scales = ring.tile([P, H], U8, name="w1_scales", align_bytes=64, bufs=6)
+            flat = grouped[:].rearrange("p t m j -> p (t m j)")
+            per = PACK // pieces
+            for u in range(pieces):
+                part = slice(u * per * P, (u + 1) * per * P)
+                nc.vector.quantize_mx(out=codes[:, part].bitcast(FP8X4), scales=scales[:, part], in_=flat[:, u * per * P * PACK:(u + 1) * per * P * PACK])
+                if e == E - 1:
+                    for t in range(u * per, (u + 1) * per):
+                        first_layer_matmul(acc[t][:], e, o, t, codes, scales)
+            return codes, scales
 
-        def second_layer(e, acc):
+        def first_layer_matmul(dst, e, o, t, codes, scales):
+            cols = slice(t * P, (t + 1) * P)
+            slots = slice(e * C, (e + 1) * C)
+            nc.tensor.matmul_mx(
+                out=dst,
+                lhsT=codes[:, cols].bitcast(FP8X4), lhsT_scale=scales[:, cols],
+                rhs=slot_words[o][:, slots].bitcast(FP8X4), rhs_scale=slot_planes[4 * o:P, slots],
+                start=(o == 0), stop=(o == PASSES - 1))
+
+        def quantise_w2(e):
             w2_grouped = ring.tile([P, N, PACK], BF16, name="w2_grouped", align_bytes=64)
             nc.scalar.copy(out=w2_grouped[:].rearrange("p (c i) j -> p c j i", i=4), in_=w2_raw[e][:].rearrange("p j (c i) -> p c j i", i=4))
             w2_codes = ring.tile([P, N], U32, name="w2_codes", align_bytes=64)
             w2_scales = ring.tile([P, N], U8, name="w2_scales", align_bytes=64)
             nc.vector.quantize_mx(out=w2_codes[:].bitcast(FP8X4), scales=w2_scales[:], in_=w2_grouped[:].rearrange("p n j -> p (n j)"))
-            h = ring.tile([P, PACK, C], BF16, name="h", align_bytes=64)
-            for t in range(PACK):
-                nc.scalar.activation(out=h[:, t, :], in_=acc[t][:], func=mybir.ActivationFunctionType.Silu)
-            h_grouped = ring.tile([P, C, PACK], BF16, name="h_grouped", align_bytes=64)
-            nc.vector.tensor_copy(out=h_grouped[:].rearrange("p (c i) t -> p c t i", i=4), in_=h[:].rearrange("p t (c i) -> p c t i", i=4))
+            return w2_codes, w2_scales
+
+        def second_layer(e, acc, w2_codes, w2_scales):
+            if e == E - 1:
+                h_grouped = keep.tile([P, C, PACK], BF16, name="h_grouped", align_bytes=64)
+                h = keep.tile([P, PACK, C], BF16, name="h", align_bytes=64)
+                for t in range(PACK):
+                    nc.scalar.activation(out=h[:, t, :], in_=acc[t][:], func=mybir.ActivationFunctionType.Silu)
+                nc.vector.tensor_copy(out=h_grouped[:].rearrange("p (c i) t -> p c t i", i=4), in_=h[:].rearrange("p t (c i) -> p c t i", i=4))
+            else:
+                h_grouped = keep.tile([P, C, PACK], BF16, name="h_grouped", tag="raw%d_0_0" % (e + 1), align_bytes=64)
+                nc.scalar.activation(out=h_grouped[:], in_=acc[:].rearrange("p t c -> p c t"), func=mybir.ActivationFunctionType.Silu)
             h_codes = ring.tile([P, C], U32, name="h_codes", align_bytes=64)
             h_scales = ring.tile([P, C], U8, name="h_scales", align_bytes=64)
             nc.vector.quantize_mx(out=h_codes[:].bitcast(FP8X4), scales=h_scales[:], in_=h_grouped[:].rearrange("p c t -> p (c t)"))
             y_ps = psum.tile([P, C], F32, name="y_ps", bufs=2)
             nc.tensor.matmul_mx(out=y_ps[:], lhsT=w2_codes[:].bitcast(FP8X4), lhsT_scale=w2_scales[:],
                                 rhs=h_codes[:].bitcast(FP8X4), rhs_scale=h_scales[:], start=True, stop=True)
-            y = ring.tile([P, C], F32, name="y")
+            return y_ps
+
+        def scatter(e, y_ps):
+            if e == E - 1:
+                y = keep.tile([P, C], F32, name="y")
+            else:
+                last = len(w1_raw[e + 1, PASSES - 1]) - 1
+                y = keep.tile([P, C], F32, name="y", tag="raw%d_%d_%d" % (e + 1, PASSES - 1, last), align_bytes=64)
             nc.scalar.copy(out=y[:], in_=y_ps[:])
             nc.vector.tensor_tensor(window[:].indirect(offsets[:, e * LIST_COLS:(e + 1) * LIST_COLS]), y[:], gate_rows[:, e * C:(e + 1) * C], mybir.AluOpType.mult)
 
         for e in range(E):
-            acc = [psum.tile([P, C], F32, name="acc%d" % t) for t in range(PACK)]
+            if e == E - 1:
+                acc = [psum.tile([P, C], F32, name="acc_last%d" % t) for t in range(PACK)]
+            else:
+                acc = psum.tile([P, PACK, C], F32, name="acc")
+            quantised = []
             for o in range(PASSES):
                 if e == 0:
                     gather_words(o)
                     if o == 0:
                         nc.vector.tensor_copy(slot_planes[:], planes[:].indirect(offsets[:]))
-                first_layer_pass(e, o, acc)
-            second_layer(e, acc)
+                quantised.append(first_layer_pass(e, o, acc))
+                if e > 0 and o == 0:
+                    y_ps = second_layer(e - 1, acc_before, w2_codes, w2_scales)
+            if e > 0:
+                scatter(e - 1, y_ps)
+            if e < E - 1:
+                for t in range(PACK):
+                    for o in range(PASSES):
+                        first_layer_matmul(acc[:, t, :], e, o, t, quantised[o][0], quantised[o][1])
+            w2_codes, w2_scales = quantise_w2(e)
+            acc_before = acc
+        scatter(E - 1, second_layer(E - 1, acc, w2_codes, w2_scales))
         nc.sync.dma_start(out=out, in_=window[:])

from contextlib import ExitStack

import concourse.mybir as mybir
from concourse.masks import make_identity

K, T, E, C, H, N = 1536, 1024, 4, 128, 512, 128
FLOPS = 2 * E * C * (K * H + H * N)

F32 = mybir.dt.float32
BF16 = mybir.dt.bfloat16
I32 = mybir.dt.int32
U32 = mybir.dt.uint32
U16 = mybir.dt.uint16
U8 = mybir.dt.uint8
FP8X4 = mybir.dt.float8_e4m3fn_x4

P = 128
PACK = 4
K_PASS = P * PACK
PASSES = K // K_PASS
SLOTS = E * C
LIST_COLS = C // 16


def tile_moe_pkd_mlp_silu_kernel(tc, x_words, x_scales, w1, w2, gate, offs, out):
    nc = tc.nc
    with ExitStack() as ctx:
        keep = ctx.enter_context(tc.tile_pool(name="keep", bufs=1))
        ring = ctx.enter_context(tc.tile_pool(name="ring", bufs=4))
        psum = ctx.enter_context(tc.psum_pool(name="psum", bufs=1))

        offsets = keep.tile([P, SLOTS // 16], U16, name="offsets")
        planes = keep.tile([P, T], U8, name="planes", align_bytes=64)
        window = keep.tile([P, T], F32, name="window")
        ident = keep.tile([P, P], F32, name="ident")
        gate_col = keep.tile([P, PACK], F32, name="gate_col")
        gate_rows = keep.tile([P, SLOTS], F32, name="gate_rows")
        words = [keep.tile([P, T], U32, name="words%d" % o, align_bytes=64) for o in range(PASSES)]
        slot_words = [keep.tile([P, SLOTS], U32, name="slot_words%d" % o, align_bytes=64) for o in range(PASSES)]
        slot_planes = keep.tile([P, SLOTS], U8, name="slot_planes", align_bytes=64)
        w1_raw = {}
        w2_raw = {}

        def load_words(o):
            nc.sync.dma_start(out=words[o][:].bitcast(I32), in_=x_words[o].rearrange("p t r -> p (t r)").bitcast(I32))

        def load_w1(e, o):
            pieces = 2 if (e, o) == (E - 1, PASSES - 1) else 1
            width = H // pieces
            rows = w1[e, o * K_PASS:(o + 1) * K_PASS, :].rearrange("(p j) c -> p j c", j=PACK)
            w1_raw[e, o] = []
            for u in range(pieces):
                raw = keep.tile([P, PACK, width], F32, name="w1_raw%d_%d_%d" % (e, o, u), tag="raw%d_%d_%d" % (e, o, u), align_bytes=64)
                nc.sync.dma_start(out=raw[:], in_=rows[:, :, u * width:(u + 1) * width])
                w1_raw[e, o].append(raw)

        def load_w2(e):
            w2_raw[e] = keep.tile([P, PACK, N], F32, name="w2_raw%d" % e)
            nc.sync.dma_start(out=w2_raw[e][:], in_=w2[e].rearrange("(p j) n -> p j n", j=PACK))

        nc.gpsimd.memset(planes[:].bitcast(I32), 0)
        nc.scalar.dma_start(out=gate_col[:], in_=gate[0:1, :].rearrange("o (p j) -> (o p) j", j=PACK))
        load_words(0)
        nc.sync.dma_start(offsets[:], offs)
        for e in range(E):
            for o in range(PASSES):
                load_w1(e, o)
                if e == 0 and o == 0:
                    for q in range(4):
                        nc.sync.dma_start(out=planes[32 * q:32 * q + 4 * PASSES, :].bitcast(I32), in_=x_scales[:, 4 * q:4 * q + 4, :].bitcast(I32))
                if e == 0 and o + 1 < PASSES:
                    load_words(o + 1)
            load_w2(e)

        nc.vector.memset(window[:], 0.0)
        make_identity(nc, ident[:])
        gate_ps = psum.tile([P, PACK, P], F32, name="gate_ps")
        for j in range(PACK):
            nc.tensor.transpose(gate_ps[:, j, :], gate_col[:, j:j + 1].to_broadcast([P, P]), ident[:])
        nc.scalar.copy(out=gate_rows[:].rearrange("p (s j) -> p s j", j=PACK), in_=gate_ps[:].rearrange("p j s -> p s j"))

        def gather_words(o):
            nc.vector.tensor_copy(slot_words[o][:], words[o][:].indirect(offsets[:]))

        def first_layer_pass(e, o, acc):
            grouped = ring.tile([P, PACK, P, PACK], BF16, name="w1_grouped", align_bytes=64)
            pieces = len(w1_raw[e, o])
            for u, raw in enumerate(w1_raw[e, o]):
                src = raw[:].rearrange("p j (m t) -> p m j t", t=PACK)
                dst = grouped[:, :, u * P // pieces:(u + 1) * P // pieces, :].rearrange("p t m j -> p m j t")
                nc.vector.tensor_copy(out=dst[:, :, :, 0:2], in_=src[:, :, :, 0:2])
                nc.scalar.copy(out=dst[:, :, :, 2:4], in_=src[:, :, :, 2:4])
            codes = ring.tile([P, H], U32, name="w1_codes", align_bytes=64, bufs=6)
            scales = ring.tile([P, H], U8, name="w1_scales", align_bytes=64, bufs=6)
            flat = grouped[:].rearrange("p t m j -> p (t m j)")
            per = PACK // pieces
            for u in range(pieces):
                part = slice(u * per * P, (u + 1) * per * P)
                nc.vector.quantize_mx(out=codes[:, part].bitcast(FP8X4), scales=scales[:, part], in_=flat[:, u * per * P * PACK:(u + 1) * per * P * PACK])
                if e == E - 1:
                    for t in range(u * per, (u + 1) * per):
                        first_layer_matmul(acc[t][:], e, o, t, codes, scales)
            return codes, scales

        def first_layer_matmul(dst, e, o, t, codes, scales):
            cols = slice(t * P, (t + 1) * P)
            slots = slice(e * C, (e + 1) * C)
            nc.tensor.matmul_mx(
                out=dst,
                lhsT=codes[:, cols].bitcast(FP8X4), lhsT_scale=scales[:, cols],
                rhs=slot_words[o][:, slots].bitcast(FP8X4), rhs_scale=slot_planes[4 * o:P, slots],
                start=(o == 0), stop=(o == PASSES - 1))

        def quantise_w2(e):
            w2_grouped = ring.tile([P, N, PACK], BF16, name="w2_grouped", align_bytes=64)
            nc.scalar.copy(out=w2_grouped[:].rearrange("p (c i) j -> p c j i", i=4), in_=w2_raw[e][:].rearrange("p j (c i) -> p c j i", i=4))
            w2_codes = ring.tile([P, N], U32, name="w2_codes", align_bytes=64)
            w2_scales = ring.tile([P, N], U8, name="w2_scales", align_bytes=64)
            nc.vector.quantize_mx(out=w2_codes[:].bitcast(FP8X4), scales=w2_scales[:], in_=w2_grouped[:].rearrange("p n j -> p (n j)"))
            return w2_codes, w2_scales

        def second_layer(e, acc, w2_codes, w2_scales):
            if e == E - 1:
                h_grouped = keep.tile([P, C, PACK], BF16, name="h_grouped", align_bytes=64)
                h = keep.tile([P, PACK, C], BF16, name="h", align_bytes=64)
                for t in range(PACK):
                    nc.scalar.activation(out=h[:, t, :], in_=acc[t][:], func=mybir.ActivationFunctionType.Silu)
                nc.vector.tensor_copy(out=h_grouped[:].rearrange("p (c i) t -> p c t i", i=4), in_=h[:].rearrange("p t (c i) -> p c t i", i=4))
            else:
                h_grouped = keep.tile([P, C, PACK], BF16, name="h_grouped", tag="raw%d_0_0" % (e + 1), align_bytes=64)
                nc.scalar.activation(out=h_grouped[:], in_=acc[:].rearrange("p t c -> p c t"), func=mybir.ActivationFunctionType.Silu)
            h_codes = ring.tile([P, C], U32, name="h_codes", align_bytes=64)
            h_scales = ring.tile([P, C], U8, name="h_scales", align_bytes=64)
            nc.vector.quantize_mx(out=h_codes[:].bitcast(FP8X4), scales=h_scales[:], in_=h_grouped[:].rearrange("p c t -> p (c t)"))
            y_ps = psum.tile([P, C], F32, name="y_ps", bufs=2)
            nc.tensor.matmul_mx(out=y_ps[:], lhsT=w2_codes[:].bitcast(FP8X4), lhsT_scale=w2_scales[:],
                                rhs=h_codes[:].bitcast(FP8X4), rhs_scale=h_scales[:], start=True, stop=True)
            return y_ps

        def scatter(e, y_ps):
            if e == E - 1:
                y = keep.tile([P, C], F32, name="y")
            else:
                last = len(w1_raw[e + 1, PASSES - 1]) - 1
                y = keep.tile([P, C], F32, name="y", tag="raw%d_%d_%d" % (e + 1, PASSES - 1, last), align_bytes=64)
            nc.scalar.copy(out=y[:], in_=y_ps[:])
            nc.vector.tensor_tensor(window[:].indirect(offsets[:, e * LIST_COLS:(e + 1) * LIST_COLS]), y[:], gate_rows[:, e * C:(e + 1) * C], mybir.AluOpType.mult)

        for e in range(E):
            if e == E - 1:
                acc = [psum.tile([P, C], F32, name="acc_last%d" % t) for t in range(PACK)]
            else:
                acc = psum.tile([P, PACK, C], F32, name="acc")
            quantised = []
            for o in range(PASSES):
                if e == 0:
                    gather_words(o)
                    if o == 0:
                        nc.vector.tensor_copy(slot_planes[:], planes[:].indirect(offsets[:]))
                quantised.append(first_layer_pass(e, o, acc))
                if e > 0 and o == 0:
                    y_ps = second_layer(e - 1, acc_before, w2_codes, w2_scales)
            if e > 0:
                scatter(e - 1, y_ps)
            if e < E - 1:
                for t in range(PACK):
                    for o in range(PASSES):
                        first_layer_matmul(acc[:, t, :], e, o, t, quantised[o][0], quantised[o][1])
            w2_codes, w2_scales = quantise_w2(e)
            acc_before = acc
        scatter(E - 1, second_layer(E - 1, acc, w2_codes, w2_scales))
        nc.sync.dma_start(out=out, in_=window[:])
